import numpy as np
import ml_dtypes


def mxq(x, axis, fmt="e4m3"):
    dtype, down = {"e4m3": (ml_dtypes.float8_e4m3fn, 7), "e5m2": (ml_dtypes.float8_e5m2, 14)}[fmt]
    v = np.moveaxis(np.asarray(x, np.float32).astype(ml_dtypes.bfloat16).astype(np.float64), axis, -1)
    blocks = v.reshape(v.shape[:-1] + (-1, 32))
    amax = np.abs(blocks).max(-1, keepdims=True)
    byte = np.maximum(np.where(amax > 0, np.frexp(amax)[1] - 1 + 127, 0) - down, 1)
    scale = np.exp2(byte - 127.0)
    codes = (blocks / scale).astype(np.float32).astype(dtype).astype(np.float64)
    return np.moveaxis((codes * scale).reshape(v.shape), -1, axis)


WIDE = False


def mx_kscale(k):
    if not WIDE:
        return np.ones(k)
    levels = np.array([10, -10, 5, -5, 0])
    if k % 512:
        return np.exp2(np.random.permutation(np.resize(levels, k // 32))).repeat(32)
    a = np.empty((k // 512, 16))
    for p in range(k // 512):
        a[p, :8] = np.random.permutation(np.resize(levels, 8))
        for g in range(8):
            far = levels[np.abs(levels - a[p, g]) >= 10]
            a[p, g + 8] = far[np.random.randint(len(far))]
    return np.exp2(a.ravel()).repeat(32)


def f64(x):
    return np.asarray(x).astype(np.float64)


def striped(idx):
    return np.tile(idx.reshape(-1, 16).T, (8, 1)).astype(np.uint16)


def unstriped(offs):
    return offs[:16].T.reshape(-1).astype(np.int64)


def striped8(idx):
    return np.concatenate([x.reshape(-1, 16).T for x in idx]).astype(np.uint16)


def runs(offs, k):
    lists = np.stack([offs[16 * r : 16 * r + 16].T.reshape(-1) for r in range(8)]).astype(np.int64)
    return lists[np.arange(k) % 512 // 64]


def pack_weight(w):
    k, n = w.shape
    w = f64(np.asarray(w, np.float32).astype(ml_dtypes.bfloat16)).reshape(k // 32, 32, n)
    amax = np.abs(w).max(1)
    byte = np.clip(np.where(amax > 0, np.frexp(amax)[1] - 1 + 127 - 7, 1), 1, 254)
    scaled = (w * np.exp2(127.0 - byte)[:, None, :]).reshape(k, n).astype(np.float32)
    words = np.ascontiguousarray(scaled.reshape(k // 512, 128, 4, n).transpose(0, 1, 3, 2)).astype(ml_dtypes.float8_e4m3fn).view(np.uint8)
    return words, np.ascontiguousarray(byte.astype(np.uint8).reshape(k // 512, 16, n))


def unpack_weight(words, scales):
    g, p, n, _ = words.shape
    vals = np.ascontiguousarray(words).view(ml_dtypes.float8_e4m3fn).astype(np.float64) * np.repeat(np.exp2(scales.astype(np.float64) - 127.0), 8, axis=1)[..., None]
    return vals.transpose(0, 1, 3, 2).reshape(g * 512, n)


K, T, S, G, H = 512, 1024, 512, 2048, 512


def setup_inputs():
    n = np.random.standard_normal
    s = mx_kscale(K)[:, None]
    packed_xT = pack_weight(n((K, T)) * s)
    packed_dT = pack_weight(n((K, G)) / s)
    return {
        "x_words": packed_xT[0],
        "x_scales": packed_xT[1],
        "d_words": packed_dT[0],
        "d_scales": packed_dT[1],
        "gs": (np.random.uniform(0.5, 1.5, (K, 1)) * s).astype(np.float32),
        "offs": striped(np.random.permutation(T)[:S]),
        "k1": striped8(np.random.randint(0, G, (8, H))),
        "n1": striped8(np.stack([np.random.permutation(S) for _ in range(8)])),
        "n2": striped8(np.stack([np.random.permutation(S) for _ in range(8)])),
        "k2": striped8(np.random.randint(0, G, (8, H))),
        "n3": striped8(np.stack([np.random.permutation(S) for _ in range(8)])),
        "n4": striped8(np.stack([np.random.permutation(S) for _ in range(8)])),
    }


def reference(x_words, x_scales, d_words, d_scales, gs, offs, k1, n1, n2, k2, n3, n4):
    d_k2 = unpack_weight(d_words, d_scales)[np.arange(K)[:, None], runs(k2, K)]
    d_k1 = unpack_weight(d_words, d_scales)[np.arange(K)[:, None], runs(k1, K)]
    xq = unpack_weight(x_words, x_scales)[:, unstriped(offs)]
    h = 0.0625 * (d_k1.T @ xq)
    ex = np.exp(0.5 * h)
    z = f64(gs) * ((2.0 * ex) / (ex + ex[np.arange(H)[:, None], runs(n1, H)] + ex[np.arange(H)[:, None], runs(n2, H)]))
    h2 = 0.0625 * ((d_k2.T @ mxq(z, 0, "e4m3")))
    st = np.maximum(h2, h2[np.arange(H)[:, None], runs(n3, H)])
    return np.minimum(st, st[np.arange(H)[:, None], runs(n4, H)])

@@ -1,0 +1,193 @@
+from contextlib import ExitStack
+
+import concourse.mybir as mybir
+
+K, T, S, G, H = 512, 1024, 512, 2048, 512
+FLOPS = 2 * 2 * K * H * S
+
+F32 = mybir.dt.float32
+BF16 = mybir.dt.bfloat16
+I32 = mybir.dt.int32
+U32 = mybir.dt.uint32
+U16 = mybir.dt.uint16
+U8 = mybir.dt.uint8
+FP8X4 = mybir.dt.float8_e4m3fn_x4
+ACT = mybir.ActivationFunctionType
+ALU = mybir.AluOpType
+
+P = 128
+PACK = 4
+CHUNKS = ((0, 256), (256, 384), (384, 512))
+
+
+def tile_picked_codesharehopmn_none_p_kernel(tc, x_words, x_scales, d_words, d_scales, gs, offs, k1, n1, n2, k2, n3, n4, out):
+    nc = tc.nc
+    with ExitStack() as ctx:
+        lists = ctx.enter_context(tc.tile_pool(name="lists", bufs=1))
+        keep = ctx.enter_context(tc.tile_pool(name="keep", bufs=1))
+        psum = ctx.enter_context(tc.psum_pool(name="psum", bufs=1))
+
+        def load_list(name, src):
+            t = lists.tile([P, S // 16], U16, name=name)
+            nc.sync.dma_start(t[:], src)
+            return t
+
+        d_scale_table = keep.tile([P, G], U8, align_bytes=64)
+        x_scale_table = keep.tile([P, T], U8, align_bytes=64)
+        nc.gpsimd.memset(d_scale_table[:].bitcast(I32), 0)
+        nc.gpsimd.dma_start(d_scale_table[0:P:8, :].bitcast(I32), d_scales[0].bitcast(I32))
+        nc.vector.memset(x_scale_table[:].bitcast(I32), 0)
+        for q in range(4):
+            nc.scalar.dma_start(x_scale_table[32 * q : 32 * q + 4, :].bitcast(I32), x_scales[0, 4 * q : 4 * q + 4, :].bitcast(I32))
+        k1_t = load_list("k1_t", k1)
+        offs_t = load_list("offs_t", offs)
+        gs_t = keep.tile([P, PACK], F32)
+        nc.sync.dma_start(gs_t[:], gs.rearrange("(p t) o -> p (t o)", t=PACK))
+        k2_t = load_list("k2_t", k2)
+        n1_t = load_list("n1_t", n1)
+        n2_t = load_list("n2_t", n2)
+        x_word_table = keep.tile([P, T], U32, align_bytes=64)
+        d_word_table = keep.tile([P, G], U32, align_bytes=64)
+        nc.sync.dma_start(x_word_table[:].bitcast(I32), x_words[0].rearrange("p n t -> p (n t)").bitcast(I32))
+        nc.sync.dma_start(d_word_table[:].bitcast(I32), d_words[0].rearrange("p n t -> p (n t)").bitcast(I32))
+        n3_t = load_list("n3_t", n3)
+        n4_t = load_list("n4_t", n4)
+
+        w1_scales = keep.tile([P, H], U8, align_bytes=64)
+        w2_scales = keep.tile([P, H], U8, align_bytes=64)
+        nc.vector.memset(w1_scales[:].bitcast(I32), 0)
+        nc.vector.memset(w2_scales[:].bitcast(I32), 0)
+        win_a = [keep.tile([P, 2 * S], F32, name="win_a%d" % t, align_bytes=64) for t in range(PACK)]
+        win_b = [keep.tile([P, 2 * S], F32, name="win_b%d" % t, align_bytes=64) for t in range(PACK)]
+        ex_twin = [win_a[t ^ 1][:, S:] for t in range(PACK)]
+
+        gs2 = keep.tile([P, PACK], F32)
+        nc.scalar.activation(gs2[:], gs_t[:], ACT.Copy, scale=2.0)
+
+        def place_scales(dst, src, queues):
+            for q in range(4):
+                queues[q].dma_start(dst[32 * q : 32 * q + 4, :].bitcast(I32), src[32 * q : 32 * q + 32 : 8, :].bitcast(I32))
+
+        picked_s1 = keep.tile([P, H], U8, align_bytes=64)
+        dealt_s1 = keep.tile([P, H], U8, align_bytes=64)
+        nc.vector.tensor_copy(picked_s1[:], d_scale_table[:].indirect(k1_t[:]))
+        nc.vector.tensor_copy(dealt_s1[:].rearrange("p (t m) -> p m t", t=PACK), picked_s1[:].rearrange("p (m t) -> p m t", t=PACK))
+        place_scales(w1_scales, dealt_s1, (nc.sync, nc.scalar, nc.sync, nc.scalar))
+        x_sc = keep.tile([P, S], U8, align_bytes=64, tag="bytes")
+        x_wd = keep.tile([P, S], U32, align_bytes=64)
+        nc.vector.tensor_copy(x_sc[:], x_scale_table[:].indirect(offs_t[:]))
+        picked_w = keep.tile([P, H], U32, align_bytes=64)
+        w1_words = keep.tile([P, H], U32, align_bytes=64)
+        w2_words = keep.tile([P, H], U32, align_bytes=64)
+        nc.vector.tensor_copy(picked_w[:], d_word_table[:].indirect(k1_t[:]))
+        nc.vector.tensor_copy(x_wd[:], x_word_table[:].indirect(offs_t[:]))
+        nc.vector.tensor_copy(w1_words[:].rearrange("p (t m) -> p m t", t=PACK), picked_w[:].rearrange("p (m t) -> p m t", t=PACK))
+
+        bank_a = [psum.tile([P, S], F32, name="bank_a%d" % t) for t in range(PACK)]
+        bank_b = [psum.tile([P, S], F32, name="bank_b%d" % t) for t in range(PACK)]
+        for t in range(PACK):
+            cols = slice(P * t, P * (t + 1))
+            nc.tensor.matmul_mx(out=bank_a[t][:], lhsT=w1_words[:, cols].bitcast(FP8X4), lhsT_scale=w1_scales[:, cols],
+                                rhs=x_wd[:].bitcast(FP8X4), rhs_scale=x_sc[:], start=True, stop=True)
+
+        nc.vector.tensor_copy(picked_w[:], d_word_table[:].indirect(k2_t[:]))
+        nc.vector.tensor_copy(w2_words[:].rearrange("p (t u r) -> p u t r", t=PACK, r=4), picked_w[:].rearrange("p (u t r) -> p u t r", t=PACK, r=4))
+        picked_s2 = keep.tile([P, H], U8, align_bytes=64, tag="bytes")
+        dealt_s2 = keep.tile([P, H], U8, align_bytes=64)
+        nc.vector.tensor_copy(picked_s2[:], d_scale_table[:].indirect(k2_t[:]))
+        nc.vector.tensor_copy(dealt_s2[:].bitcast(I32).rearrange("p (t u) -> p u t", t=PACK), picked_s2[:].bitcast(I32).rearrange("p (u t) -> p u t", t=PACK))
+        place_scales(w2_scales, dealt_s2, (nc.sync, nc.sync, nc.sync, nc.sync))
+
+        ex_gs = keep.tile([P, PACK, S], F32, align_bytes=64)
+        den = [keep.tile([P, S], F32, name="den%d" % t, align_bytes=64) for t in range(PACK)]
+        root = [keep.tile([P, S], F32, name="root%d" % t, align_bytes=64) for t in range(PACK)]
+        inv = [keep.tile([P, PACK, b - a], F32, name="inv%d" % c, align_bytes=64) for c, (a, b) in enumerate(CHUNKS)]
+        for t in range(PACK):
+            nc.scalar.activation(win_a[t][:, :S], bank_a[t][:], ACT.Exp, scale=0.03125)
+            if t < 2:
+                nc.scalar.activation(ex_twin[t], bank_a[t][:], ACT.Exp, scale=0.03125)
+            else:
+                nc.sync.dma_start(ex_twin[t], win_a[t][:, :S])
+        for t in range(PACK):
+            nc.scalar.activation(ex_gs[:, t, :], win_a[t][:, :S], ACT.Copy, scale=gs2[:, t : t + 1])
+        def add_first(t):
+            nc.vector.tensor_tensor(win_b[t][:, S:], win_a[t][:].indirect(n1_t[:]), ex_twin[t], ALU.add)
+
+        def add_second(t):
+            halves = ((0, S),) if t < PACK - 1 else ((0, S // 2), (S // 2, S))
+            for a, b in halves:
+                nc.vector.tensor_tensor(den[t][:, a:b], win_a[t][:].indirect(n2_t[:, a // 16 : b // 16]), win_b[t][:, S + a : S + b], ALU.add)
+                nc.scalar.activation(root[t][:, a:b], den[t][:, a:b], ACT.Abs_reciprocal_sqrt)
+                for c, (ca, cb) in enumerate(CHUNKS):
+                    if a <= ca and cb <= b:
+                        nc.scalar.activation(inv[c][:, t, :], root[t][:, ca:cb], ACT.Square)
+
+        for t in range(0, PACK, 2):
+            for step in (add_first, add_second):
+                step(t)
+                step(t + 1)
+
+        z_bf = [keep.tile([P, PACK * (b - a)], BF16, name="z_bf%d" % c, align_bytes=64) for c, (a, b) in enumerate(CHUNKS)]
+        z_wd = [keep.tile([P, b - a], U32, name="z_wd%d" % c, align_bytes=64) for c, (a, b) in enumerate(CHUNKS)]
+        z_sc = [keep.tile([P, b - a], U8, name="z_sc%d" % c, align_bytes=64) for c, (a, b) in enumerate(CHUNKS)]
+
+        def weigh(c):
+            a, b = CHUNKS[c]
+            nc.vector.tensor_tensor(z_bf[c][:].rearrange("p (j i t) -> p j t i", i=4, t=PACK),
+                                    ex_gs[:, :, a:b].rearrange("p t (j i) -> p j t i", i=4),
+                                    inv[c][:].rearrange("p t (j i) -> p j t i", i=4), ALU.mult)
+
+        def multiply(c):
+            a, b = CHUNKS[c]
+            nc.vector.quantize_mx(out=z_wd[c][:].bitcast(FP8X4), scales=z_sc[c][:], in_=z_bf[c][:])
+            banks = bank_a if c == len(CHUNKS) - 1 else bank_b
+            for t in range(PACK):
+                cols = slice(P * t, P * (t + 1))
+                nc.tensor.matmul_mx(out=banks[t][:, a:b], lhsT=w2_words[:, cols].bitcast(FP8X4), lhsT_scale=w2_scales[:, cols],
+                                    rhs=z_wd[c][:].bitcast(FP8X4), rhs_scale=z_sc[c][:], start=True, stop=True)
+
+        weigh(0)
+        for c in range(1, len(CHUNKS)):
+            weigh(c)
+            multiply(c - 1)
+        multiply(len(CHUNKS) - 1)
+
+        last = CHUNKS[-1][0]
+        for t in range(PACK):
+            nc.scalar.activation(win_a[t][:, :last], bank_b[t][:, :last], ACT.Copy, scale=0.0625)
+            nc.scalar.activation(win_a[t][:, last:S], bank_a[t][:, last:S], ACT.Copy, scale=0.0625)
+        fetched = [keep.tile([P, S], F32, name="fetched%d" % t, align_bytes=64) for t in range(PACK)]
+        result = [keep.tile([P, S], F32, name="result%d" % t, align_bytes=64) for t in range(PACK)]
+        out_t = out.rearrange("(u t r) j -> t u r j", t=PACK, r=4)
+
+        def fetch3(t):
+            nc.vector.tensor_copy(fetched[t][:], win_a[t][:].indirect(n3_t[:]))
+
+        def larger(t):
+            nc.vector.tensor_tensor(win_b[t][:, :S], fetched[t][:], win_a[t][:, :S], ALU.max)
+
+        def fetch4(t, a=0, b=S):
+            nc.vector.tensor_copy(den[t][:, a:b], win_b[t][:].indirect(n4_t[:, a // 16 : b // 16]))
+
+        def smaller(t, a=0, b=S):
+            nc.vector.tensor_tensor(result[t][:, a:b], den[t][:, a:b], win_b[t][:, a:b], ALU.min)
+            nc.sync.dma_start(out_t[t, :, :, a:b], result[t][:, a:b])
+
+        fetch3(0)
+        fetch3(1)
+        larger(0)
+        larger(1)
+        fetch4(0)
+        fetch4(1)
+        fetch3(2)
+        smaller(0)
+        fetch3(3)
+        smaller(1)
+        larger(2)
+        larger(3)
+        fetch4(2)
+        fetch4(3, 0, S // 2)
+        smaller(2)
+        fetch4(3, S // 2, S)
+        smaller(3, 0, S // 2)
+        smaller(3, S // 2, S)

@@ -1,6 +1,7 @@
 from contextlib import ExitStack
 
 import concourse.mybir as mybir
+from concourse.masks import make_identity
 
 K, T, S, G, H = 512, 1024, 512, 2048, 512
 FLOPS = 2 * 2 * K * H * S
@@ -17,7 +18,7 @@ ALU = mybir.AluOpType
 
 P = 128
 PACK = 4
-CHUNKS = ((0, 256), (256, 384), (384, 512))
+CHUNKS = ((0, 128), (128, 256), (256, 384), (384, 512))
 
 
 def tile_picked_codesharehopmn_none_p_kernel(tc, x_words, x_scales, d_words, d_scales, gs, offs, k1, n1, n2, k2, n3, n4, out):
@@ -33,23 +34,23 @@ def tile_picked_codesharehopmn_none_p_kernel(tc, x_words, x_scales, d_words, d_s
             return t
 
         d_scale_table = keep.tile([P, G], U8, align_bytes=64)
-        x_scale_table = keep.tile([P, T], U8, align_bytes=64)
+        x_scale_table = keep.tile([P, T], U8, align_bytes=64, tag="early")
         nc.gpsimd.memset(d_scale_table[:].bitcast(I32), 0)
         nc.gpsimd.dma_start(d_scale_table[0:P:8, :].bitcast(I32), d_scales[0].bitcast(I32))
         nc.vector.memset(x_scale_table[:].bitcast(I32), 0)
         for q in range(4):
             nc.scalar.dma_start(x_scale_table[32 * q : 32 * q + 4, :].bitcast(I32), x_scales[0, 4 * q : 4 * q + 4, :].bitcast(I32))
-        k1_t = load_list("k1_t", k1)
         offs_t = load_list("offs_t", offs)
+        k1_t = load_list("k1_t", k1)
+        x_word_table = keep.tile([P, T], U32, align_bytes=64, tag="x_words")
+        d_word_table = keep.tile([P, G], U32, align_bytes=64)
+        nc.sync.dma_start(x_word_table[:].bitcast(I32), x_words[0].rearrange("p n t -> p (n t)").bitcast(I32))
         gs_t = keep.tile([P, PACK], F32)
         nc.sync.dma_start(gs_t[:], gs.rearrange("(p t) o -> p (t o)", t=PACK))
         k2_t = load_list("k2_t", k2)
         n1_t = load_list("n1_t", n1)
-        n2_t = load_list("n2_t", n2)
-        x_word_table = keep.tile([P, T], U32, align_bytes=64)
-        d_word_table = keep.tile([P, G], U32, align_bytes=64)
-        nc.sync.dma_start(x_word_table[:].bitcast(I32), x_words[0].rearrange("p n t -> p (n t)").bitcast(I32))
         nc.sync.dma_start(d_word_table[:].bitcast(I32), d_words[0].rearrange("p n t -> p (n t)").bitcast(I32))
+        n2_t = load_list("n2_t", n2)
         n3_t = load_list("n3_t", n3)
         n4_t = load_list("n4_t", n4)
 
@@ -68,23 +69,26 @@ def tile_picked_codesharehopmn_none_p_kernel(tc, x_words, x_scales, d_words, d_s
             for q in range(4):
                 queues[q].dma_start(dst[32 * q : 32 * q + 4, :].bitcast(I32), src[32 * q : 32 * q + 32 : 8, :].bitcast(I32))
 
+        x_wd = keep.tile([P, S], U32, align_bytes=64)
+        nc.vector.tensor_copy(x_wd[:], x_word_table[:].indirect(offs_t[:]))
         picked_s1 = keep.tile([P, H], U8, align_bytes=64)
         dealt_s1 = keep.tile([P, H], U8, align_bytes=64)
         nc.vector.tensor_copy(picked_s1[:], d_scale_table[:].indirect(k1_t[:]))
         nc.vector.tensor_copy(dealt_s1[:].rearrange("p (t m) -> p m t", t=PACK), picked_s1[:].rearrange("p (m t) -> p m t", t=PACK))
         place_scales(w1_scales, dealt_s1, (nc.sync, nc.scalar, nc.sync, nc.scalar))
-        x_sc = keep.tile([P, S], U8, align_bytes=64, tag="bytes")
-        x_wd = keep.tile([P, S], U32, align_bytes=64)
-        nc.vector.tensor_copy(x_sc[:], x_scale_table[:].indirect(offs_t[:]))
-        picked_w = keep.tile([P, H], U32, align_bytes=64)
-        w1_words = keep.tile([P, H], U32, align_bytes=64)
-        w2_words = keep.tile([P, H], U32, align_bytes=64)
+        picked_w = keep.tile([P, H], U32, align_bytes=64, tag="picked")
         nc.vector.tensor_copy(picked_w[:], d_word_table[:].indirect(k1_t[:]))
-        nc.vector.tensor_copy(x_wd[:], x_word_table[:].indirect(offs_t[:]))
+        x_sc = keep.tile([P, S], U8, align_bytes=64)
+        nc.vector.tensor_copy(x_sc[:], x_scale_table[:].indirect(offs_t[:]))
+        w1_words = keep.tile([P, H], U32, align_bytes=64, tag="early")
+        w2_words = keep.tile([P, H], U32, align_bytes=64)
         nc.vector.tensor_copy(w1_words[:].rearrange("p (t m) -> p m t", t=PACK), picked_w[:].rearrange("p (m t) -> p m t", t=PACK))
 
-        bank_a = [psum.tile([P, S], F32, name="bank_a%d" % t) for t in range(PACK)]
-        bank_b = [psum.tile([P, S], F32, name="bank_b%d" % t) for t in range(PACK)]
+        ident = keep.tile([P, P], F32, align_bytes=64, tag="x_words")
+        make_identity(nc, ident[:])
+        bank = [psum.tile([P, S], F32, name="bank%d" % b) for b in range(8)]
+        bank_a = bank[:PACK]
+        h2_bank = ((4, 4, 5, 6), (7, 7, 0, 0), (1, 1, 1, 1), (2, 2, 2, 2))
         for t in range(PACK):
             cols = slice(P * t, P * (t + 1))
             nc.tensor.matmul_mx(out=bank_a[t][:], lhsT=w1_words[:, cols].bitcast(FP8X4), lhsT_scale=w1_scales[:, cols],
@@ -92,7 +96,7 @@ def tile_picked_codesharehopmn_none_p_kernel(tc, x_words, x_scales, d_words, d_s
 
         nc.vector.tensor_copy(picked_w[:], d_word_table[:].indirect(k2_t[:]))
         nc.vector.tensor_copy(w2_words[:].rearrange("p (t u r) -> p u t r", t=PACK, r=4), picked_w[:].rearrange("p (u t r) -> p u t r", t=PACK, r=4))
-        picked_s2 = keep.tile([P, H], U8, align_bytes=64, tag="bytes")
+        picked_s2 = keep.tile([P, H], U8, align_bytes=64, tag="picked")
         dealt_s2 = keep.tile([P, H], U8, align_bytes=64)
         nc.vector.tensor_copy(picked_s2[:], d_scale_table[:].indirect(k2_t[:]))
         nc.vector.tensor_copy(dealt_s2[:].bitcast(I32).rearrange("p (t u) -> p u t", t=PACK), picked_s2[:].bitcast(I32).rearrange("p (u t) -> p u t", t=PACK))
@@ -101,7 +105,8 @@ def tile_picked_codesharehopmn_none_p_kernel(tc, x_words, x_scales, d_words, d_s
         ex_gs = keep.tile([P, PACK, S], F32, align_bytes=64)
         den = [keep.tile([P, S], F32, name="den%d" % t, align_bytes=64) for t in range(PACK)]
         root = [keep.tile([P, S], F32, name="root%d" % t, align_bytes=64) for t in range(PACK)]
-        inv = [keep.tile([P, PACK, b - a], F32, name="inv%d" % c, align_bytes=64) for c, (a, b) in enumerate(CHUNKS)]
+        halves = ((0, S // 2), (S // 2, S))
+        inv = [keep.tile([P, PACK, S // 2], F32, name="inv%d" % i, align_bytes=64) for i in range(2)]
         for t in range(PACK):
             nc.scalar.activation(win_a[t][:, :S], bank_a[t][:], ACT.Exp, scale=0.03125)
             if t < 2:
@@ -114,13 +119,12 @@ def tile_picked_codesharehopmn_none_p_kernel(tc, x_words, x_scales, d_words, d_s
             nc.vector.tensor_tensor(win_b[t][:, S:], win_a[t][:].indirect(n1_t[:]), ex_twin[t], ALU.add)
 
         def add_second(t):
-            halves = ((0, S),) if t < PACK - 1 else ((0, S // 2), (S // 2, S))
-            for a, b in halves:
+            for a, b in ((0, S),) if t < PACK - 1 else halves:
                 nc.vector.tensor_tensor(den[t][:, a:b], win_a[t][:].indirect(n2_t[:, a // 16 : b // 16]), win_b[t][:, S + a : S + b], ALU.add)
                 nc.scalar.activation(root[t][:, a:b], den[t][:, a:b], ACT.Abs_reciprocal_sqrt)
-                for c, (ca, cb) in enumerate(CHUNKS):
-                    if a <= ca and cb <= b:
-                        nc.scalar.activation(inv[c][:, t, :], root[t][:, ca:cb], ACT.Square)
+                for i, (ha, hb) in enumerate(halves):
+                    if a <= ha and hb <= b:
+                        nc.scalar.activation(inv[i][:, t, :], root[t][:, ha:hb], ACT.Square)
 
         for t in range(0, PACK, 2):
             for step in (add_first, add_second):
@@ -128,23 +132,30 @@ def tile_picked_codesharehopmn_none_p_kernel(tc, x_words, x_scales, d_words, d_s
                 step(t + 1)
 
         z_bf = [keep.tile([P, PACK * (b - a)], BF16, name="z_bf%d" % c, align_bytes=64) for c, (a, b) in enumerate(CHUNKS)]
-        z_wd = [keep.tile([P, b - a], U32, name="z_wd%d" % c, align_bytes=64) for c, (a, b) in enumerate(CHUNKS)]
-        z_sc = [keep.tile([P, b - a], U8, name="z_sc%d" % c, align_bytes=64) for c, (a, b) in enumerate(CHUNKS)]
+        z_wd = [keep.tile([P, S // 2], U32, name="z_wd%d" % i, align_bytes=64) for i in range(2)]
+        z_sc = [keep.tile([P, S // 2], U8, name="z_sc%d" % i, align_bytes=64) for i in range(2)]
 
         def weigh(c):
             a, b = CHUNKS[c]
+            i, lo = divmod(a, S // 2)
             nc.vector.tensor_tensor(z_bf[c][:].rearrange("p (j i t) -> p j t i", i=4, t=PACK),
                                     ex_gs[:, :, a:b].rearrange("p t (j i) -> p j t i", i=4),
-                                    inv[c][:].rearrange("p t (j i) -> p j t i", i=4), ALU.mult)
+                                    inv[i][:, :, lo : lo + b - a].rearrange("p t (j i) -> p j t i", i=4), ALU.mult)
+
+        def product(t, a, b):
+            i, lo = divmod(a, S // 2)
+            cols = slice(P * t, P * (t + 1))
+            nc.tensor.matmul_mx(out=bank[h2_bank[t][a // P]][:, a:b], lhsT=w2_words[:, cols].bitcast(FP8X4), lhsT_scale=w2_scales[:, cols],
+                                rhs=z_wd[i][:, lo : lo + b - a].bitcast(FP8X4), rhs_scale=z_sc[i][:, lo : lo + b - a], start=True, stop=True)
 
         def multiply(c):
             a, b = CHUNKS[c]
-            nc.vector.quantize_mx(out=z_wd[c][:].bitcast(FP8X4), scales=z_sc[c][:], in_=z_bf[c][:])
-            banks = bank_a if c == len(CHUNKS) - 1 else bank_b
-            for t in range(PACK):
-                cols = slice(P * t, P * (t + 1))
-                nc.tensor.matmul_mx(out=banks[t][:, a:b], lhsT=w2_words[:, cols].bitcast(FP8X4), lhsT_scale=w2_scales[:, cols],
-                                    rhs=z_wd[c][:].bitcast(FP8X4), rhs_scale=z_sc[c][:], start=True, stop=True)
+            i, lo = divmod(a, S // 2)
+            nc.vector.quantize_mx(out=z_wd[i][:, lo : lo + b - a].bitcast(FP8X4), scales=z_sc[i][:, lo : lo + b - a], in_=z_bf[c][:])
+            product(0, a, b)
+            if b == halves[i][1]:
+                for t in range(1, PACK):
+                    product(t, halves[i][0], b)
 
         weigh(0)
         for c in range(1, len(CHUNKS)):
@@ -152,42 +163,77 @@ def tile_picked_codesharehopmn_none_p_kernel(tc, x_words, x_scales, d_words, d_s
             multiply(c - 1)
         multiply(len(CHUNKS) - 1)
 
-        last = CHUNKS[-1][0]
-        for t in range(PACK):
-            nc.scalar.activation(win_a[t][:, :last], bank_b[t][:, :last], ACT.Copy, scale=0.0625)
-            nc.scalar.activation(win_a[t][:, last:S], bank_a[t][:, last:S], ACT.Copy, scale=0.0625)
-        fetched = [keep.tile([P, S], F32, name="fetched%d" % t, align_bytes=64) for t in range(PACK)]
-        result = [keep.tile([P, S], F32, name="result%d" % t, align_bytes=64) for t in range(PACK)]
+        def plane(name):
+            return keep.tile([P, S], F32, name=name, align_bytes=64)
+
         out_t = out.rearrange("(u t r) j -> t u r j", t=PACK, r=4)
+        h2 = [win_a[t][:, :S] for t in range(PACK)]
+        st = [win_b[t][:, :S] for t in range(PACK)]
+        fetched = [plane("fetched%d" % t) for t in range(PACK)]
+        result = [plane("result%d" % t) for t in range(PACK)]
+        twin = [plane("twin%d" % t) for t in range(3)]
+        turned = [plane("turned%d" % t) for t in range(3)]
+        diff = [plane("diff0")[:], st[3], result[0][:]]
+        excess = [[st[1][:, : S // 2], st[2][:, : S // 2]]]
+        for t in (1, 2):
+            whole = plane("excess%d" % t)
+            excess.append([whole[:, a:b] for a, b in halves])
 
-        def fetch3(t):
-            nc.vector.tensor_copy(fetched[t][:], win_a[t][:].indirect(n3_t[:]))
+        def leave_banks(t, sign, dsts):
+            for b in sorted(set(h2_bank[t]), key=h2_bank[t].index):
+                cs = [c for c in range(len(CHUNKS)) if h2_bank[t][c] == b]
+                cols = slice(CHUNKS[cs[0]][0], CHUNKS[cs[-1]][1])
+                for dst in dsts:
+                    nc.scalar.activation(dst[:, cols], bank[b][:, cols], ACT.Copy, scale=sign * 0.0625)
 
-        def larger(t):
-            nc.vector.tensor_tensor(win_b[t][:, :S], fetched[t][:], win_a[t][:, :S], ALU.max)
+        def add_turned(b, x, y):
+            for j in range(0, S, P):
+                nc.tensor.matmul(bank[b][:, j : j + P], x[:, j : j + P], ident[:], is_transpose=True, start=True, stop=False)
+                nc.tensor.matmul(bank[b][:, j : j + P], y[j // (S // 2)][:, j % (S // 2) : j % (S // 2) + P], ident[:], is_transpose=True, start=False, stop=True)
 
-        def fetch4(t, a=0, b=S):
-            nc.vector.tensor_copy(den[t][:, a:b], win_b[t][:].indirect(n4_t[:, a // 16 : b // 16]))
+        def turn_back(t, src_bank, dst_bank):
+            nc.scalar.copy(turned[t][:], bank[src_bank][:])
+            for j in range(0, S, P):
+                nc.tensor.transpose(bank[dst_bank][:, j : j + P], turned[t][:, j : j + P], ident[:])
 
-        def smaller(t, a=0, b=S):
-            nc.vector.tensor_tensor(result[t][:, a:b], den[t][:, a:b], win_b[t][:, a:b], ALU.min)
+        def positive_part(t):
+            for (a, b), dst in zip(halves, excess[t]):
+                nc.scalar.activation(dst, diff[t][:, a:b], ACT.Relu)
+
+        def store(t, a=0, b=S):
             nc.sync.dma_start(out_t[t, :, :, a:b], result[t][:, a:b])
 
-        fetch3(0)
-        fetch3(1)
-        larger(0)
-        larger(1)
-        fetch4(0)
-        fetch4(1)
-        fetch3(2)
-        smaller(0)
-        fetch3(3)
-        smaller(1)
-        larger(2)
-        larger(3)
-        fetch4(2)
-        fetch4(3, 0, S // 2)
-        smaller(2)
-        fetch4(3, S // 2, S)
-        smaller(3, 0, S // 2)
-        smaller(3, S // 2, S)
+        leave_banks(0, 1.0, (h2[0], twin[0]))
+        leave_banks(1, -1.0, (h2[1],))
+        leave_banks(2, -1.0, (h2[2],))
+        nc.vector.tensor_tensor(diff[0], win_a[0][:].indirect(n3_t[:]), twin[0][:], ALU.subtract)
+        for t in (1, 2):
+            nc.vector.tensor_copy(fetched[t][:], win_a[t][:].indirect(n3_t[:]))
+        positive_part(0)
+        add_turned(3, h2[0], excess[0])
+        leave_banks(3, 1.0, (h2[3],))
+        turn_back(0, 3, 4)
+        for t in (1, 2):
+            nc.vector.tensor_tensor(st[t], fetched[t][:], h2[t], ALU.min)
+            nc.scalar.copy(twin[t][:], st[t])
+        nc.scalar.copy(st[0], bank[4][:])
+        for t in (1, 2):
+            nc.vector.tensor_tensor(diff[t], win_b[t][:].indirect(n4_t[:]), twin[t][:], ALU.subtract)
+        nc.vector.tensor_copy(fetched[3][:], win_a[3][:].indirect(n3_t[:]))
+        nc.vector.tensor_copy(fetched[0][:], win_b[0][:].indirect(n4_t[:]))
+        for t in (1, 2):
+            positive_part(t)
+            add_turned(3 + 2 * t, st[t], excess[t])
+        nc.vector.tensor_tensor(st[3], fetched[3][:], h2[3], ALU.max)
+        nc.vector.tensor_tensor(result[0][:], fetched[0][:], st[0], ALU.min)
+        store(0)
+        for t in (1, 2):
+            turn_back(t, 3 + 2 * t, (4 + 2 * t) % 8)
+        for t in (1, 2):
+            nc.scalar.activation(result[t][:], bank[(4 + 2 * t) % 8][:], ACT.Copy, scale=-1.0)
+            store(t)
+        for a, b in halves:
+            nc.vector.tensor_copy(den[3][:, a:b], win_b[3][:].indirect(n4_t[:, a // 16 : b // 16]))
+        for a, b in halves:
+            nc.vector.tensor_tensor(result[3][:, a:b], den[3][:, a:b], st[3][:, a:b], ALU.min)
+            store(3, a, b)

@@ -55,12 +55,9 @@ def tile_picked_codesharehopmn_none_p_kernel(tc, x_words, x_scales, d_words, d_s
         n4_t = load_list("n4_t", n4)
 
         w1_scales = keep.tile([P, H], U8, align_bytes=64)
-        w2_scales = keep.tile([P, H], U8, align_bytes=64)
         nc.vector.memset(w1_scales[:].bitcast(I32), 0)
-        nc.vector.memset(w2_scales[:].bitcast(I32), 0)
         win_a = [keep.tile([P, 2 * S], F32, name="win_a%d" % t, align_bytes=64) for t in range(PACK)]
         win_b = [keep.tile([P, 2 * S], F32, name="win_b%d" % t, align_bytes=64) for t in range(PACK)]
-        ex_twin = [win_a[t ^ 1][:, S:] for t in range(PACK)]
 
         gs2 = keep.tile([P, PACK], F32)
         nc.scalar.activation(gs2[:], gs_t[:], ACT.Copy, scale=2.0)
@@ -88,7 +85,7 @@ def tile_picked_codesharehopmn_none_p_kernel(tc, x_words, x_scales, d_words, d_s
         make_identity(nc, ident[:])
         bank = [psum.tile([P, S], F32, name="bank%d" % b) for b in range(8)]
         bank_a = bank[:PACK]
-        h2_bank = ((4, 4, 5, 6), (7, 7, 0, 0), (1, 1, 1, 1), (2, 2, 2, 2))
+        h2_bank = ((7, 7, 7, 7), (4, 4, 6, 5), (1, 1, 1, 1), (2, 2, 2, 2))
         for t in range(PACK):
             cols = slice(P * t, P * (t + 1))
             nc.tensor.matmul_mx(out=bank_a[t][:], lhsT=w1_words[:, cols].bitcast(FP8X4), lhsT_scale=w1_scales[:, cols],
@@ -100,101 +97,130 @@ def tile_picked_codesharehopmn_none_p_kernel(tc, x_words, x_scales, d_words, d_s
         dealt_s2 = keep.tile([P, H], U8, align_bytes=64)
         nc.vector.tensor_copy(picked_s2[:], d_scale_table[:].indirect(k2_t[:]))
         nc.vector.tensor_copy(dealt_s2[:].bitcast(I32).rearrange("p (t u) -> p u t", t=PACK), picked_s2[:].bitcast(I32).rearrange("p (u t) -> p u t", t=PACK))
-        place_scales(w2_scales, dealt_s2, (nc.sync, nc.sync, nc.sync, nc.sync))
-
-        ex_gs = keep.tile([P, PACK, S], F32, align_bytes=64)
-        den = [keep.tile([P, S], F32, name="den%d" % t, align_bytes=64) for t in range(PACK)]
-        root = [keep.tile([P, S], F32, name="root%d" % t, align_bytes=64) for t in range(PACK)]
-        halves = ((0, S // 2), (S // 2, S))
-        inv = [keep.tile([P, PACK, S // 2], F32, name="inv%d" % i, align_bytes=64) for i in range(2)]
-        for t in range(PACK):
-            nc.scalar.activation(win_a[t][:, :S], bank_a[t][:], ACT.Exp, scale=0.03125)
-            if t < 2:
-                nc.scalar.activation(ex_twin[t], bank_a[t][:], ACT.Exp, scale=0.03125)
-            else:
-                nc.sync.dma_start(ex_twin[t], win_a[t][:, :S])
-        for t in range(PACK):
-            nc.scalar.activation(ex_gs[:, t, :], win_a[t][:, :S], ACT.Copy, scale=gs2[:, t : t + 1])
-        def add_first(t):
-            nc.vector.tensor_tensor(win_b[t][:, S:], win_a[t][:].indirect(n1_t[:]), ex_twin[t], ALU.add)
-
-        def add_second(t):
-            for a, b in ((0, S),) if t < PACK - 1 else halves:
-                nc.vector.tensor_tensor(den[t][:, a:b], win_a[t][:].indirect(n2_t[:, a // 16 : b // 16]), win_b[t][:, S + a : S + b], ALU.add)
-                nc.scalar.activation(root[t][:, a:b], den[t][:, a:b], ACT.Abs_reciprocal_sqrt)
-                for i, (ha, hb) in enumerate(halves):
-                    if a <= ha and hb <= b:
-                        nc.scalar.activation(inv[i][:, t, :], root[t][:, ha:hb], ACT.Square)
-
-        for t in range(0, PACK, 2):
-            for step in (add_first, add_second):
-                step(t)
-                step(t + 1)
-
-        z_bf = [keep.tile([P, PACK * (b - a)], BF16, name="z_bf%d" % c, align_bytes=64) for c, (a, b) in enumerate(CHUNKS)]
-        z_wd = [keep.tile([P, S // 2], U32, name="z_wd%d" % i, align_bytes=64) for i in range(2)]
-        z_sc = [keep.tile([P, S // 2], U8, name="z_sc%d" % i, align_bytes=64) for i in range(2)]
-
-        def weigh(c):
-            a, b = CHUNKS[c]
-            i, lo = divmod(a, S // 2)
-            nc.vector.tensor_tensor(z_bf[c][:].rearrange("p (j i t) -> p j t i", i=4, t=PACK),
-                                    ex_gs[:, :, a:b].rearrange("p t (j i) -> p j t i", i=4),
-                                    inv[i][:, :, lo : lo + b - a].rearrange("p t (j i) -> p j t i", i=4), ALU.mult)
-
-        def product(t, a, b):
-            i, lo = divmod(a, S // 2)
-            cols = slice(P * t, P * (t + 1))
-            nc.tensor.matmul_mx(out=bank[h2_bank[t][a // P]][:, a:b], lhsT=w2_words[:, cols].bitcast(FP8X4), lhsT_scale=w2_scales[:, cols],
-                                rhs=z_wd[i][:, lo : lo + b - a].bitcast(FP8X4), rhs_scale=z_sc[i][:, lo : lo + b - a], start=True, stop=True)
-
-        def multiply(c):
-            a, b = CHUNKS[c]
-            i, lo = divmod(a, S // 2)
-            nc.vector.quantize_mx(out=z_wd[i][:, lo : lo + b - a].bitcast(FP8X4), scales=z_sc[i][:, lo : lo + b - a], in_=z_bf[c][:])
-            product(0, a, b)
-            if b == halves[i][1]:
-                for t in range(1, PACK):
-                    product(t, halves[i][0], b)
-
-        weigh(0)
-        for c in range(1, len(CHUNKS)):
-            weigh(c)
-            multiply(c - 1)
-        multiply(len(CHUNKS) - 1)
 
         def plane(name):
             return keep.tile([P, S], F32, name=name, align_bytes=64)
 
+        def add_turned(place, terms):
+            for j in range(0, S, P):
+                for n, term in enumerate(terms):
+                    nc.tensor.matmul(place(j), term(j), ident[:], is_transpose=True, start=n == 0, stop=n == len(terms) - 1)
+
+        def block_of(x):
+            return lambda j: x[:, j : j + P]
+
+        def turn(src, b):
+            for j in range(0, S, P):
+                nc.tensor.transpose(bank[b][:, j : j + P], src[:, j : j + P], ident[:])
+
+        halves = ((0, S // 2), (S // 2, S))
+        ex0 = plane("ex0")
+        ex = [ex0[:], win_a[1][:, :S], win_a[2][:, :S], win_a[3][:, S:]]
+        ex_twin = {1: win_a[2][:, S:], 2: win_a[1][:, S:]}
+        den = [None, win_a[0][:, S:], plane("den2"), keep.tile([P, S], F32, name="den3", align_bytes=64, tag="late")]
+        root = [win_a[3][:, :S], plane("root_b")[:]]
+        half_root = {1: root[1][:, : S // 2], 2: root[1][:, S // 2 :]}
+        inv_turned = keep.tile([P, 2, S], F32, align_bytes=64)
+        inv = [inv_turned[:, 0, :], plane("inv1")[:], plane("inv2")[:], inv_turned[:, 1, :]]
+        for t in range(3):
+            nc.scalar.activation(ex[t], bank_a[t][:], ACT.Exp, scale=0.03125)
+            if t in ex_twin:
+                nc.sync.dma_start(ex_twin[t], ex[t])
+        nc.scalar.activation(win_a[3][:, :S], bank_a[3][:], ACT.Copy, scale=0.03125)
+        nc.scalar.activation(ex[3], bank_a[3][:], ACT.Exp, scale=0.03125)
+        nc.scalar.activation(win_b[3][:, S:], win_a[3][:].indirect(n1_t[:]), ACT.Exp)
+        nc.scalar.activation(den[3][:], win_a[3][:].indirect(n2_t[:]), ACT.Exp)
+
+        for i, (a, b) in enumerate(halves):
+            nc.vector.tensor_copy(win_b[1 + i][:, S + a : S + b], ex0[:].indirect(n1_t[:, a // 16 : b // 16]))
+        for i, (a, b) in enumerate(halves):
+            nc.vector.tensor_tensor(win_b[0][:, S + a : S + b], ex0[:].indirect(n2_t[:, a // 16 : b // 16]), win_b[1 + i][:, S + a : S + b], ALU.add)
+
+        def shared_place(slot):
+            def place(j):
+                i, lo = divmod(j, S // 2)
+                return bank[4 + 2 * i][:, slot * (S // 2) + lo : slot * (S // 2) + lo + P]
+
+            return place
+
+        add_turned(shared_place(0), [block_of(ex[0]), block_of(win_b[0][:, S:])])
+        add_turned(shared_place(1), [block_of(ex[3]), block_of(win_b[3][:, S:]), block_of(den[3])])
+        for i in range(2):
+            nc.scalar.activation(root[i], bank[4 + 2 * i][:], ACT.Abs_reciprocal_sqrt)
+            turn(root[i], 5 + 2 * i)
+        for i, (a, b) in enumerate(halves):
+            nc.scalar.activation(inv_turned[:, :, a:b], bank[5 + 2 * i][:].rearrange("p (s j) -> p s j", s=2), ACT.Square)
+        w2_scales = keep.tile([P, H], U8, align_bytes=64, tag="late")
+        nc.gpsimd.memset(w2_scales[:].bitcast(I32), 0)
+        place_scales(w2_scales, dealt_s2, (nc.sync, nc.sync, nc.sync, nc.sync))
+
+        for t in (1, 2):
+            nc.vector.tensor_tensor(win_b[t][:, S:], win_a[t][:].indirect(n1_t[:]), ex_twin[t], ALU.add)
+        for a, b in halves:
+            for t in (1, 2):
+                nc.vector.tensor_tensor(den[t][:, a:b], win_a[t][:].indirect(n2_t[:, a // 16 : b // 16]), win_b[t][:, S + a : S + b], ALU.add)
+                nc.scalar.activation(half_root[t], den[t][:, a:b], ACT.Abs_reciprocal_sqrt)
+                nc.scalar.activation(inv[t][:, a:b], half_root[t], ACT.Square)
+
+        z_planes = [keep.tile([P, PACK, S // 2], BF16, name="z_planes%d" % i, align_bytes=64) for i in range(2)]
+        for ts in ((0, 3), (1, 2)):
+            for i, (a, b) in enumerate(halves):
+                for t in ts:
+                    nc.vector.scalar_tensor_tensor(z_planes[i][:, t, :], ex[t][:, a:b], gs2[:, t : t + 1], inv[t][:, a:b], ALU.mult, ALU.mult)
+
+        z_bf = [keep.tile([P, PACK * (b - a)], BF16, name="z_bf%d" % c, align_bytes=64) for c, (a, b) in enumerate(CHUNKS)]
+        z_wd = keep.tile([P, S], U32, align_bytes=64)
+        z_sc = keep.tile([P, S], U8, align_bytes=64)
+
+        def weave(c):
+            a, b = CHUNKS[c]
+            i, lo = divmod(a, S // 2)
+            copy = nc.scalar.copy if c < len(CHUNKS) - 1 else nc.vector.tensor_copy
+            copy(z_bf[c][:].rearrange("p (j i t) -> p j t i", i=4, t=PACK), z_planes[i][:, :, lo : lo + b - a].rearrange("p t (j i) -> p j t i", i=4))
+
+        def product(t, a, b):
+            cols = slice(P * t, P * (t + 1))
+            nc.tensor.matmul_mx(out=bank[h2_bank[t][a // P]][:, a:b], lhsT=w2_words[:, cols].bitcast(FP8X4), lhsT_scale=w2_scales[:, cols],
+                                rhs=z_wd[:, a:b].bitcast(FP8X4), rhs_scale=z_sc[:, a:b], start=True, stop=True)
+
+        def multiply(c):
+            a, b = CHUNKS[c]
+            nc.vector.quantize_mx(out=z_wd[:, a:b].bitcast(FP8X4), scales=z_sc[:, a:b], in_=z_bf[c][:])
+            product(1, a, b)
+
+        for c in range(len(CHUNKS)):
+            weave(c)
+        for c in (0, 1, 3, 2):
+            multiply(c)
+        for t in (0, 2, 3):
+            product(t, 0, S)
+
         out_t = out.rearrange("(u t r) j -> t u r j", t=PACK, r=4)
         h2 = [win_a[t][:, :S] for t in range(PACK)]
         st = [win_b[t][:, :S] for t in range(PACK)]
-        fetched = [plane("fetched%d" % t) for t in range(PACK)]
         result = [plane("result%d" % t) for t in range(PACK)]
-        twin = [plane("twin%d" % t) for t in range(3)]
-        turned = [plane("turned%d" % t) for t in range(3)]
-        diff = [plane("diff0")[:], st[3], result[0][:]]
+        twin = [plane("twin0")[:], plane("twin1")[:], st[3]]
+        fetched = [plane("fetched%d" % t)[:] for t in range(3)] + [twin[1]]
+        fetched_last = win_b[0][:, S:]
+        turned = [fetched[2], plane("turned1"), plane("turned2")]
+        diff = [plane("diff%d" % t) for t in range(3)]
         excess = [[st[1][:, : S // 2], st[2][:, : S // 2]]]
-        for t in (1, 2):
-            whole = plane("excess%d" % t)
+        for whole in (plane("excess1"), turned[0]):
             excess.append([whole[:, a:b] for a, b in halves])
 
         def leave_banks(t, sign, dsts):
-            for b in sorted(set(h2_bank[t]), key=h2_bank[t].index):
+            for b in sorted(set(h2_bank[t])):
                 cs = [c for c in range(len(CHUNKS)) if h2_bank[t][c] == b]
                 cols = slice(CHUNKS[cs[0]][0], CHUNKS[cs[-1]][1])
                 for dst in dsts:
                     nc.scalar.activation(dst[:, cols], bank[b][:, cols], ACT.Copy, scale=sign * 0.0625)
 
-        def add_turned(b, x, y):
-            for j in range(0, S, P):
-                nc.tensor.matmul(bank[b][:, j : j + P], x[:, j : j + P], ident[:], is_transpose=True, start=True, stop=False)
-                nc.tensor.matmul(bank[b][:, j : j + P], y[j // (S // 2)][:, j % (S // 2) : j % (S // 2) + P], ident[:], is_transpose=True, start=False, stop=True)
+        def block_of_halves(y):
+            return lambda j: y[j // (S // 2)][:, j % (S // 2) : j % (S // 2) + P]
 
         def turn_back(t, src_bank, dst_bank):
             nc.scalar.copy(turned[t][:], bank[src_bank][:])
-            for j in range(0, S, P):
-                nc.tensor.transpose(bank[dst_bank][:, j : j + P], turned[t][:, j : j + P], ident[:])
+            turn(turned[t], dst_bank)
 
         def positive_part(t):
             for (a, b), dst in zip(halves, excess[t]):
@@ -203,37 +229,38 @@ def tile_picked_codesharehopmn_none_p_kernel(tc, x_words, x_scales, d_words, d_s
         def store(t, a=0, b=S):
             nc.sync.dma_start(out_t[t, :, :, a:b], result[t][:, a:b])
 
-        leave_banks(0, 1.0, (h2[0], twin[0]))
         leave_banks(1, -1.0, (h2[1],))
+        leave_banks(0, 1.0, (h2[0], twin[0]))
         leave_banks(2, -1.0, (h2[2],))
-        nc.vector.tensor_tensor(diff[0], win_a[0][:].indirect(n3_t[:]), twin[0][:], ALU.subtract)
-        for t in (1, 2):
-            nc.vector.tensor_copy(fetched[t][:], win_a[t][:].indirect(n3_t[:]))
+        nc.vector.tensor_copy(fetched[1], win_a[1][:].indirect(n3_t[:]))
+        nc.vector.tensor_tensor(diff[0][:], win_a[0][:].indirect(n3_t[:]), twin[0], ALU.subtract)
+        nc.vector.tensor_copy(fetched[2], win_a[2][:].indirect(n3_t[:]))
         positive_part(0)
-        add_turned(3, h2[0], excess[0])
+        add_turned(block_of(bank[3]), [block_of(h2[0]), block_of_halves(excess[0])])
         leave_banks(3, 1.0, (h2[3],))
+        for t in (1, 2):
+            nc.vector.tensor_tensor(st[t], fetched[t], h2[t], ALU.min)
+            nc.scalar.copy(twin[t], st[t])
         turn_back(0, 3, 4)
-        for t in (1, 2):
-            nc.vector.tensor_tensor(st[t], fetched[t][:], h2[t], ALU.min)
-            nc.scalar.copy(twin[t][:], st[t])
         nc.scalar.copy(st[0], bank[4][:])
-        for t in (1, 2):
-            nc.vector.tensor_tensor(diff[t], win_b[t][:].indirect(n4_t[:]), twin[t][:], ALU.subtract)
-        nc.vector.tensor_copy(fetched[3][:], win_a[3][:].indirect(n3_t[:]))
-        nc.vector.tensor_copy(fetched[0][:], win_b[0][:].indirect(n4_t[:]))
+        nc.vector.tensor_tensor(diff[1][:], win_b[1][:].indirect(n4_t[:]), twin[1], ALU.subtract)
+        nc.vector.tensor_copy(fetched[3], win_a[3][:].indirect(n3_t[:]))
+        nc.vector.tensor_tensor(diff[2][:], win_b[2][:].indirect(n4_t[:]), twin[2], ALU.subtract)
+        nc.vector.tensor_tensor(st[3], fetched[3], h2[3], ALU.max)
         for t in (1, 2):
             positive_part(t)
-            add_turned(3 + 2 * t, st[t], excess[t])
-        nc.vector.tensor_tensor(st[3], fetched[3][:], h2[3], ALU.max)
-        nc.vector.tensor_tensor(result[0][:], fetched[0][:], st[0], ALU.min)
-        store(0)
+            add_turned(block_of(bank[3 + 2 * t]), [block_of(st[t]), block_of_halves(excess[t])])
         for t in (1, 2):
             turn_back(t, 3 + 2 * t, (4 + 2 * t) % 8)
         for t in (1, 2):
             nc.scalar.activation(result[t][:], bank[(4 + 2 * t) % 8][:], ACT.Copy, scale=-1.0)
             store(t)
+        nc.vector.tensor_copy(fetched[0], win_b[0][:].indirect(n4_t[:]))
+        for i, (a, b) in enumerate(halves):
+            nc.vector.tensor_copy(fetched_last[:, a:b], win_b[3][:].indirect(n4_t[:, a // 16 : b // 16]))
+            if i == 0:
+                nc.vector.tensor_tensor(result[0][:], fetched[0], st[0], ALU.min)
+                store(0)
         for a, b in halves:
-            nc.vector.tensor_copy(den[3][:, a:b], win_b[3][:].indirect(n4_t[:, a // 16 : b // 16]))
-        for a, b in halves:
-            nc.vector.tensor_tensor(result[3][:, a:b], den[3][:, a:b], st[3][:, a:b], ALU.min)
+            nc.vector.tensor_tensor(result[3][:, a:b], fetched_last[:, a:b], st[3][:, a:b], ALU.min)
             store(3, a, b)

@@ -18,7 +18,14 @@ ALU = mybir.AluOpType
 
 P = 128
 PACK = 4
-CHUNKS = ((0, 128), (128, 256), (256, 384), (384, 512))
+PER_COLUMN = 16
+LINE = 4
+HALF = S // 2
+HALVES = ((0, HALF), (HALF, S))
+QUARTERS = tuple((a, a + P) for a in range(0, S, P))
+H_SCALE = 0.0625
+EXP_SCALE = 0.5 * H_SCALE
+H2_BANK = ((7, 7, 7, 7), (4, 4, 6, 5), (1, 1, 1, 1), (2, 2, 2, 2))
 
 
 def tile_picked_codesharehopmn_none_p_kernel(tc, x_words, x_scales, d_words, d_scales, gs, offs, k1, n1, n2, k2, n3, n4, out):
@@ -29,27 +36,33 @@ def tile_picked_codesharehopmn_none_p_kernel(tc, x_words, x_scales, d_words, d_s
         psum = ctx.enter_context(tc.psum_pool(name="psum", bufs=1))
 
         def load_list(name, src):
-            t = lists.tile([P, S // 16], U16, name=name)
-            nc.sync.dma_start(t[:], src)
-            return t
+            held = lists.tile([P, S // PER_COLUMN], U16, name=name)
+            nc.sync.dma_start(held[:], src)
+            return held
+
+        def entries(list_tile, a, b):
+            return list_tile[:, a // PER_COLUMN : b // PER_COLUMN]
+
+        def as_words(packed):
+            return packed[0].rearrange("p n t -> p (n t)").bitcast(I32)
 
         d_scale_table = keep.tile([P, G], U8, align_bytes=64)
         x_scale_table = keep.tile([P, T], U8, align_bytes=64, tag="early")
+        x_word_table = keep.tile([P, T], U32, align_bytes=64, tag="x_words")
+        d_word_table = keep.tile([P, G], U32, align_bytes=64)
+        gs_t = keep.tile([P, PACK], F32)
         nc.gpsimd.memset(d_scale_table[:].bitcast(I32), 0)
-        nc.gpsimd.dma_start(d_scale_table[0:P:8, :].bitcast(I32), d_scales[0].bitcast(I32))
+        nc.gpsimd.dma_start(x_word_table[:].bitcast(I32), as_words(x_words))
+        nc.gpsimd.dma_start(d_word_table[:].bitcast(I32), as_words(d_words))
+        nc.gpsimd.dma_start(gs_t[:], gs.rearrange("(p t) o -> p (t o)", t=PACK))
+        nc.scalar.dma_start(d_scale_table[0:P:8, :].bitcast(I32), d_scales[0].bitcast(I32))
         nc.vector.memset(x_scale_table[:].bitcast(I32), 0)
         for q in range(4):
             nc.scalar.dma_start(x_scale_table[32 * q : 32 * q + 4, :].bitcast(I32), x_scales[0, 4 * q : 4 * q + 4, :].bitcast(I32))
-        offs_t = load_list("offs_t", offs)
         k1_t = load_list("k1_t", k1)
-        x_word_table = keep.tile([P, T], U32, align_bytes=64, tag="x_words")
-        d_word_table = keep.tile([P, G], U32, align_bytes=64)
-        nc.sync.dma_start(x_word_table[:].bitcast(I32), x_words[0].rearrange("p n t -> p (n t)").bitcast(I32))
-        gs_t = keep.tile([P, PACK], F32)
-        nc.sync.dma_start(gs_t[:], gs.rearrange("(p t) o -> p (t o)", t=PACK))
+        offs_t = load_list("offs_t", offs)
         k2_t = load_list("k2_t", k2)
         n1_t = load_list("n1_t", n1)
-        nc.sync.dma_start(d_word_table[:].bitcast(I32), d_words[0].rearrange("p n t -> p (n t)").bitcast(I32))
         n2_t = load_list("n2_t", n2)
         n3_t = load_list("n3_t", n3)
         n4_t = load_list("n4_t", n4)
@@ -63,20 +76,20 @@ def tile_picked_codesharehopmn_none_p_kernel(tc, x_words, x_scales, d_words, d_s
         nc.scalar.activation(gs2[:], gs_t[:], ACT.Copy, scale=2.0)
 
         def place_scales(dst, src, queues):
-            for q in range(4):
-                queues[q].dma_start(dst[32 * q : 32 * q + 4, :].bitcast(I32), src[32 * q : 32 * q + 32 : 8, :].bitcast(I32))
+            for q, queue in enumerate(queues):
+                queue.dma_start(dst[32 * q : 32 * q + 4, :].bitcast(I32), src[32 * q : 32 * q + 32 : 8, :].bitcast(I32))
 
         x_wd = keep.tile([P, S], U32, align_bytes=64)
-        nc.vector.tensor_copy(x_wd[:], x_word_table[:].indirect(offs_t[:]))
         picked_s1 = keep.tile([P, H], U8, align_bytes=64)
         dealt_s1 = keep.tile([P, H], U8, align_bytes=64)
         nc.vector.tensor_copy(picked_s1[:], d_scale_table[:].indirect(k1_t[:]))
         nc.vector.tensor_copy(dealt_s1[:].rearrange("p (t m) -> p m t", t=PACK), picked_s1[:].rearrange("p (m t) -> p m t", t=PACK))
-        place_scales(w1_scales, dealt_s1, (nc.sync, nc.scalar, nc.sync, nc.scalar))
-        picked_w = keep.tile([P, H], U32, align_bytes=64, tag="picked")
-        nc.vector.tensor_copy(picked_w[:], d_word_table[:].indirect(k1_t[:]))
+        place_scales(w1_scales, dealt_s1, (nc.sync,) * PACK)
+        nc.vector.tensor_copy(x_wd[:], x_word_table[:].indirect(offs_t[:]))
         x_sc = keep.tile([P, S], U8, align_bytes=64)
         nc.vector.tensor_copy(x_sc[:], x_scale_table[:].indirect(offs_t[:]))
+        picked_w = keep.tile([P, H], U32, align_bytes=64, tag="picked")
+        nc.vector.tensor_copy(picked_w[:], d_word_table[:].indirect(k1_t[:]))
         w1_words = keep.tile([P, H], U32, align_bytes=64, tag="early")
         w2_words = keep.tile([P, H], U32, align_bytes=64)
         nc.vector.tensor_copy(w1_words[:].rearrange("p (t m) -> p m t", t=PACK), picked_w[:].rearrange("p (m t) -> p m t", t=PACK))
@@ -84,15 +97,13 @@ def tile_picked_codesharehopmn_none_p_kernel(tc, x_words, x_scales, d_words, d_s
         ident = keep.tile([P, P], F32, align_bytes=64, tag="x_words")
         make_identity(nc, ident[:])
         bank = [psum.tile([P, S], F32, name="bank%d" % b) for b in range(8)]
-        bank_a = bank[:PACK]
-        h2_bank = ((7, 7, 7, 7), (4, 4, 6, 5), (1, 1, 1, 1), (2, 2, 2, 2))
         for t in range(PACK):
             cols = slice(P * t, P * (t + 1))
-            nc.tensor.matmul_mx(out=bank_a[t][:], lhsT=w1_words[:, cols].bitcast(FP8X4), lhsT_scale=w1_scales[:, cols],
+            nc.tensor.matmul_mx(out=bank[t][:], lhsT=w1_words[:, cols].bitcast(FP8X4), lhsT_scale=w1_scales[:, cols],
                                 rhs=x_wd[:].bitcast(FP8X4), rhs_scale=x_sc[:], start=True, stop=True)
 
         nc.vector.tensor_copy(picked_w[:], d_word_table[:].indirect(k2_t[:]))
-        nc.vector.tensor_copy(w2_words[:].rearrange("p (t u r) -> p u t r", t=PACK, r=4), picked_w[:].rearrange("p (u t r) -> p u t r", t=PACK, r=4))
+        nc.vector.tensor_copy(w2_words[:].rearrange("p (t u r) -> p u t r", t=PACK, r=LINE), picked_w[:].rearrange("p (u t r) -> p u t r", t=PACK, r=LINE))
         picked_s2 = keep.tile([P, H], U8, align_bytes=64, tag="picked")
         dealt_s2 = keep.tile([P, H], U8, align_bytes=64)
         nc.vector.tensor_copy(picked_s2[:], d_scale_table[:].indirect(k2_t[:]))
@@ -101,132 +112,128 @@ def tile_picked_codesharehopmn_none_p_kernel(tc, x_words, x_scales, d_words, d_s
         def plane(name):
             return keep.tile([P, S], F32, name=name, align_bytes=64)
 
-        def add_turned(place, terms):
-            for j in range(0, S, P):
-                for n, term in enumerate(terms):
-                    nc.tensor.matmul(place(j), term(j), ident[:], is_transpose=True, start=n == 0, stop=n == len(terms) - 1)
+        def blocks(x):
+            return [x[:, a:b] for a, b in QUARTERS]
 
-        def block_of(x):
-            return lambda j: x[:, j : j + P]
+        def blocks_of_halves(pair):
+            return [half[:, a : a + P] for half in pair for a in range(0, HALF, P)]
+
+        def add_turned(places, terms):
+            for j, place in enumerate(places):
+                for n, term in enumerate(terms):
+                    nc.tensor.matmul(place, term[j], ident[:], is_transpose=True, start=n == 0, stop=n == len(terms) - 1)
 
         def turn(src, b):
-            for j in range(0, S, P):
-                nc.tensor.transpose(bank[b][:, j : j + P], src[:, j : j + P], ident[:])
+            for block, place in zip(blocks(src), blocks(bank[b])):
+                nc.tensor.transpose(place, block, ident[:])
 
-        halves = ((0, S // 2), (S // 2, S))
         ex0 = plane("ex0")
+        h3 = win_a[3][:, :S]
         ex = [ex0[:], win_a[1][:, :S], win_a[2][:, :S], win_a[3][:, S:]]
         ex_twin = {1: win_a[2][:, S:], 2: win_a[1][:, S:]}
-        den = [None, win_a[0][:, S:], plane("den2"), keep.tile([P, S], F32, name="den3", align_bytes=64, tag="late")]
-        root = [win_a[3][:, :S], plane("root_b")[:]]
-        half_root = {1: root[1][:, : S // 2], 2: root[1][:, S // 2 :]}
+        first_sum = {t: win_b[t][:, S:] for t in (1, 2)}
+        ex0_both = win_b[0][:, S:]
+        ex0_n1 = [first_sum[1][:, :HALF], first_sum[2][:, HALF:]]
+        ex3_n1 = win_b[3][:, S:]
+        den = {1: win_a[0][:, S:], 2: plane("den2")}
+        ex3_n2 = keep.tile([P, S], F32, align_bytes=64, tag="late")
+        root = [h3, plane("root_b")[:]]
+        half_root = {1: root[1][:, :HALF], 2: root[1][:, HALF:]}
         inv_turned = keep.tile([P, 2, S], F32, align_bytes=64)
         inv = [inv_turned[:, 0, :], plane("inv1")[:], plane("inv2")[:], inv_turned[:, 1, :]]
         for t in range(3):
-            nc.scalar.activation(ex[t], bank_a[t][:], ACT.Exp, scale=0.03125)
+            nc.scalar.activation(ex[t], bank[t][:], ACT.Exp, scale=EXP_SCALE)
             if t in ex_twin:
                 nc.sync.dma_start(ex_twin[t], ex[t])
-        nc.scalar.activation(win_a[3][:, :S], bank_a[3][:], ACT.Copy, scale=0.03125)
-        nc.scalar.activation(ex[3], bank_a[3][:], ACT.Exp, scale=0.03125)
-        nc.scalar.activation(win_b[3][:, S:], win_a[3][:].indirect(n1_t[:]), ACT.Exp)
-        nc.scalar.activation(den[3][:], win_a[3][:].indirect(n2_t[:]), ACT.Exp)
+        nc.scalar.activation(h3, bank[3][:], ACT.Copy, scale=EXP_SCALE)
+        nc.scalar.activation(ex[3], bank[3][:], ACT.Exp, scale=EXP_SCALE)
+        nc.scalar.activation(ex3_n1, win_a[3][:].indirect(n1_t[:]), ACT.Exp)
+        nc.scalar.activation(ex3_n2[:], win_a[3][:].indirect(n2_t[:]), ACT.Exp)
 
-        for i, (a, b) in enumerate(halves):
-            nc.vector.tensor_copy(win_b[1 + i][:, S + a : S + b], ex0[:].indirect(n1_t[:, a // 16 : b // 16]))
-        for i, (a, b) in enumerate(halves):
-            nc.vector.tensor_tensor(win_b[0][:, S + a : S + b], ex0[:].indirect(n2_t[:, a // 16 : b // 16]), win_b[1 + i][:, S + a : S + b], ALU.add)
+        for (a, b), dst in zip(HALVES, ex0_n1):
+            nc.vector.tensor_copy(dst, ex0[:].indirect(entries(n1_t, a, b)))
+        for (a, b), src in zip(HALVES, ex0_n1):
+            nc.vector.tensor_tensor(ex0_both[:, a:b], ex0[:].indirect(entries(n2_t, a, b)), src, ALU.add)
 
-        def shared_place(slot):
-            def place(j):
-                i, lo = divmod(j, S // 2)
-                return bank[4 + 2 * i][:, slot * (S // 2) + lo : slot * (S // 2) + lo + P]
+        sum_banks = (4, 6)
+        add_turned(blocks_of_halves([bank[b][:, :HALF] for b in sum_banks]), [blocks(ex[0]), blocks(ex0_both)])
+        add_turned(blocks_of_halves([bank[b][:, HALF:] for b in sum_banks]), [blocks(ex[3]), blocks(ex3_n1), blocks(ex3_n2)])
+        for i, b in enumerate(sum_banks):
+            nc.scalar.activation(root[i], bank[b][:], ACT.Abs_reciprocal_sqrt)
+            turn(root[i], b + 1)
+        for (lo, hi), b in zip(HALVES, sum_banks):
+            nc.scalar.activation(inv_turned[:, :, lo:hi], bank[b + 1][:].rearrange("p (s j) -> p s j", s=2), ACT.Square)
 
-            return place
-
-        add_turned(shared_place(0), [block_of(ex[0]), block_of(win_b[0][:, S:])])
-        add_turned(shared_place(1), [block_of(ex[3]), block_of(win_b[3][:, S:]), block_of(den[3])])
-        for i in range(2):
-            nc.scalar.activation(root[i], bank[4 + 2 * i][:], ACT.Abs_reciprocal_sqrt)
-            turn(root[i], 5 + 2 * i)
-        for i, (a, b) in enumerate(halves):
-            nc.scalar.activation(inv_turned[:, :, a:b], bank[5 + 2 * i][:].rearrange("p (s j) -> p s j", s=2), ACT.Square)
         w2_scales = keep.tile([P, H], U8, align_bytes=64, tag="late")
         nc.gpsimd.memset(w2_scales[:].bitcast(I32), 0)
-        place_scales(w2_scales, dealt_s2, (nc.sync, nc.sync, nc.sync, nc.sync))
+        place_scales(w2_scales, dealt_s2, (nc.sync,) * PACK)
 
         for t in (1, 2):
-            nc.vector.tensor_tensor(win_b[t][:, S:], win_a[t][:].indirect(n1_t[:]), ex_twin[t], ALU.add)
-        for a, b in halves:
+            nc.vector.tensor_tensor(first_sum[t], win_a[t][:].indirect(n1_t[:]), ex_twin[t], ALU.add)
+        for a, b in HALVES:
             for t in (1, 2):
-                nc.vector.tensor_tensor(den[t][:, a:b], win_a[t][:].indirect(n2_t[:, a // 16 : b // 16]), win_b[t][:, S + a : S + b], ALU.add)
+                nc.vector.tensor_tensor(den[t][:, a:b], win_a[t][:].indirect(entries(n2_t, a, b)), first_sum[t][:, a:b], ALU.add)
                 nc.scalar.activation(half_root[t], den[t][:, a:b], ACT.Abs_reciprocal_sqrt)
                 nc.scalar.activation(inv[t][:, a:b], half_root[t], ACT.Square)
 
-        z_planes = [keep.tile([P, PACK, S // 2], BF16, name="z_planes%d" % i, align_bytes=64) for i in range(2)]
-        for ts in ((0, 3), (1, 2)):
-            for i, (a, b) in enumerate(halves):
-                for t in ts:
+        z_planes = [keep.tile([P, PACK, HALF], BF16, name="z_planes%d" % i, align_bytes=64) for i in range(2)]
+        for pair in ((0, 3), (1, 2)):
+            for i, (a, b) in enumerate(HALVES):
+                for t in pair:
                     nc.vector.scalar_tensor_tensor(z_planes[i][:, t, :], ex[t][:, a:b], gs2[:, t : t + 1], inv[t][:, a:b], ALU.mult, ALU.mult)
 
-        z_bf = [keep.tile([P, PACK * (b - a)], BF16, name="z_bf%d" % c, align_bytes=64) for c, (a, b) in enumerate(CHUNKS)]
+        z_bf = [keep.tile([P, PACK * P], BF16, name="z_bf%d" % c, align_bytes=64) for c in range(len(QUARTERS))]
         z_wd = keep.tile([P, S], U32, align_bytes=64)
         z_sc = keep.tile([P, S], U8, align_bytes=64)
 
-        def weave(c):
-            a, b = CHUNKS[c]
-            i, lo = divmod(a, S // 2)
-            copy = nc.scalar.copy if c < len(CHUNKS) - 1 else nc.vector.tensor_copy
-            copy(z_bf[c][:].rearrange("p (j i t) -> p j t i", i=4, t=PACK), z_planes[i][:, :, lo : lo + b - a].rearrange("p t (j i) -> p j t i", i=4))
-
         def product(t, a, b):
             cols = slice(P * t, P * (t + 1))
-            nc.tensor.matmul_mx(out=bank[h2_bank[t][a // P]][:, a:b], lhsT=w2_words[:, cols].bitcast(FP8X4), lhsT_scale=w2_scales[:, cols],
+            nc.tensor.matmul_mx(out=bank[H2_BANK[t][a // P]][:, a:b], lhsT=w2_words[:, cols].bitcast(FP8X4), lhsT_scale=w2_scales[:, cols],
                                 rhs=z_wd[:, a:b].bitcast(FP8X4), rhs_scale=z_sc[:, a:b], start=True, stop=True)
 
-        def multiply(c):
-            a, b = CHUNKS[c]
+        for c, (a, b) in enumerate(QUARTERS):
+            i, lo = divmod(a, HALF)
+            copy = nc.scalar.copy if b < S else nc.vector.tensor_copy
+            copy(z_bf[c][:].rearrange("p (j i t) -> p j t i", i=LINE, t=PACK), z_planes[i][:, :, lo : lo + P].rearrange("p t (j i) -> p j t i", i=LINE))
+        for c in (0, 1, 3, 2):
+            a, b = QUARTERS[c]
             nc.vector.quantize_mx(out=z_wd[:, a:b].bitcast(FP8X4), scales=z_sc[:, a:b], in_=z_bf[c][:])
             product(1, a, b)
-
-        for c in range(len(CHUNKS)):
-            weave(c)
-        for c in (0, 1, 3, 2):
-            multiply(c)
         for t in (0, 2, 3):
             product(t, 0, S)
 
-        out_t = out.rearrange("(u t r) j -> t u r j", t=PACK, r=4)
+        out_t = out.rearrange("(u t r) j -> t u r j", t=PACK, r=LINE)
         h2 = [win_a[t][:, :S] for t in range(PACK)]
         st = [win_b[t][:, :S] for t in range(PACK)]
         result = [plane("result%d" % t) for t in range(PACK)]
         twin = [plane("twin0")[:], plane("twin1")[:], st[3]]
         fetched = [plane("fetched%d" % t)[:] for t in range(3)] + [twin[1]]
         fetched_last = win_b[0][:, S:]
-        turned = [fetched[2], plane("turned1"), plane("turned2")]
+        turned = [fetched[2], plane("turned1")[:], plane("turned2")[:]]
         diff = [plane("diff%d" % t) for t in range(3)]
-        excess = [[st[1][:, : S // 2], st[2][:, : S // 2]]]
+        excess = [[st[1][:, :HALF], st[2][:, :HALF]]]
         for whole in (plane("excess1"), turned[0]):
-            excess.append([whole[:, a:b] for a, b in halves])
+            excess.append([whole[:, a:b] for a, b in HALVES])
+        turned_bank = (3, 5, 7)
+        back_bank = (4, 6, 0)
 
         def leave_banks(t, sign, dsts):
-            for b in sorted(set(h2_bank[t])):
-                cs = [c for c in range(len(CHUNKS)) if h2_bank[t][c] == b]
-                cols = slice(CHUNKS[cs[0]][0], CHUNKS[cs[-1]][1])
+            for b in sorted(set(H2_BANK[t])):
+                mine = [quarter for quarter, its_bank in zip(QUARTERS, H2_BANK[t]) if its_bank == b]
+                cols = slice(mine[0][0], mine[-1][1])
                 for dst in dsts:
-                    nc.scalar.activation(dst[:, cols], bank[b][:, cols], ACT.Copy, scale=sign * 0.0625)
+                    nc.scalar.activation(dst[:, cols], bank[b][:, cols], ACT.Copy, scale=sign * H_SCALE)
 
-        def block_of_halves(y):
-            return lambda j: y[j // (S // 2)][:, j % (S // 2) : j % (S // 2) + P]
-
-        def turn_back(t, src_bank, dst_bank):
-            nc.scalar.copy(turned[t][:], bank[src_bank][:])
-            turn(turned[t], dst_bank)
-
-        def positive_part(t):
-            for (a, b), dst in zip(halves, excess[t]):
+        def add_excess(t, base):
+            for (a, b), dst in zip(HALVES, excess[t]):
                 nc.scalar.activation(dst, diff[t][:, a:b], ACT.Relu)
+            add_turned(blocks(bank[turned_bank[t]]), [blocks(base), blocks_of_halves(excess[t])])
 
-        def store(t, a=0, b=S):
+        def turn_back(t):
+            nc.scalar.copy(turned[t], bank[turned_bank[t]][:])
+            turn(turned[t], back_bank[t])
+
+        def store(t, a, b):
             nc.sync.dma_start(out_t[t, :, :, a:b], result[t][:, a:b])
 
         leave_banks(1, -1.0, (h2[1],))
@@ -235,32 +242,30 @@ def tile_picked_codesharehopmn_none_p_kernel(tc, x_words, x_scales, d_words, d_s
         nc.vector.tensor_copy(fetched[1], win_a[1][:].indirect(n3_t[:]))
         nc.vector.tensor_tensor(diff[0][:], win_a[0][:].indirect(n3_t[:]), twin[0], ALU.subtract)
         nc.vector.tensor_copy(fetched[2], win_a[2][:].indirect(n3_t[:]))
-        positive_part(0)
-        add_turned(block_of(bank[3]), [block_of(h2[0]), block_of_halves(excess[0])])
+        add_excess(0, h2[0])
         leave_banks(3, 1.0, (h2[3],))
         for t in (1, 2):
             nc.vector.tensor_tensor(st[t], fetched[t], h2[t], ALU.min)
             nc.scalar.copy(twin[t], st[t])
-        turn_back(0, 3, 4)
-        nc.scalar.copy(st[0], bank[4][:])
+        turn_back(0)
+        nc.scalar.copy(st[0], bank[back_bank[0]][:])
         nc.vector.tensor_tensor(diff[1][:], win_b[1][:].indirect(n4_t[:]), twin[1], ALU.subtract)
         nc.vector.tensor_copy(fetched[3], win_a[3][:].indirect(n3_t[:]))
         nc.vector.tensor_tensor(diff[2][:], win_b[2][:].indirect(n4_t[:]), twin[2], ALU.subtract)
         nc.vector.tensor_tensor(st[3], fetched[3], h2[3], ALU.max)
         for t in (1, 2):
-            positive_part(t)
-            add_turned(block_of(bank[3 + 2 * t]), [block_of(st[t]), block_of_halves(excess[t])])
+            add_excess(t, st[t])
         for t in (1, 2):
-            turn_back(t, 3 + 2 * t, (4 + 2 * t) % 8)
+            turn_back(t)
         for t in (1, 2):
-            nc.scalar.activation(result[t][:], bank[(4 + 2 * t) % 8][:], ACT.Copy, scale=-1.0)
-            store(t)
+            nc.scalar.activation(result[t][:], bank[back_bank[t]][:], ACT.Copy, scale=-1.0)
+            store(t, 0, S)
+
         nc.vector.tensor_copy(fetched[0], win_b[0][:].indirect(n4_t[:]))
-        for i, (a, b) in enumerate(halves):
-            nc.vector.tensor_copy(fetched_last[:, a:b], win_b[3][:].indirect(n4_t[:, a // 16 : b // 16]))
-            if i == 0:
-                nc.vector.tensor_tensor(result[0][:], fetched[0], st[0], ALU.min)
-                store(0)
-        for a, b in halves:
+        nc.vector.tensor_copy(fetched_last[:, :HALF], win_b[3][:].indirect(entries(n4_t, 0, HALF)))
+        nc.vector.tensor_tensor(result[0][:], fetched[0], st[0], ALU.min)
+        store(0, 0, S)
+        nc.vector.tensor_copy(fetched_last[:, HALF:], win_b[3][:].indirect(entries(n4_t, HALF, S)))
+        for a, b in HALVES:
             nc.vector.tensor_tensor(result[3][:, a:b], fetched_last[:, a:b], st[3][:, a:b], ALU.min)
             store(3, a, b)

from contextlib import ExitStack

import concourse.mybir as mybir
from concourse.masks import make_identity

K, T, S, G, H = 512, 1024, 512, 2048, 512
FLOPS = 2 * 2 * K * H * S

F32 = mybir.dt.float32
BF16 = mybir.dt.bfloat16
I32 = mybir.dt.int32
U32 = mybir.dt.uint32
U16 = mybir.dt.uint16
U8 = mybir.dt.uint8
FP8X4 = mybir.dt.float8_e4m3fn_x4
ACT = mybir.ActivationFunctionType
ALU = mybir.AluOpType

P = 128
PACK = 4
PER_COLUMN = 16
LINE = 4
HALF = S // 2
HALVES = ((0, HALF), (HALF, S))
QUARTERS = tuple((a, a + P) for a in range(0, S, P))
H_SCALE = 0.0625
EXP_SCALE = 0.5 * H_SCALE
H2_BANK = ((7, 7, 7, 7), (4, 4, 6, 5), (1, 1, 1, 1), (2, 2, 2, 2))


def tile_picked_codesharehopmn_none_p_kernel(tc, x_words, x_scales, d_words, d_scales, gs, offs, k1, n1, n2, k2, n3, n4, out):
    nc = tc.nc
    with ExitStack() as ctx:
        lists = ctx.enter_context(tc.tile_pool(name="lists", bufs=1))
        keep = ctx.enter_context(tc.tile_pool(name="keep", bufs=1))
        psum = ctx.enter_context(tc.psum_pool(name="psum", bufs=1))

        def load_list(name, src):
            held = lists.tile([P, S // PER_COLUMN], U16, name=name)
            nc.sync.dma_start(held[:], src)
            return held

        def entries(list_tile, a, b):
            return list_tile[:, a // PER_COLUMN : b // PER_COLUMN]

        def as_words(packed):
            return packed[0].rearrange("p n t -> p (n t)").bitcast(I32)

        d_scale_table = keep.tile([P, G], U8, align_bytes=64)
        x_scale_table = keep.tile([P, T], U8, align_bytes=64, tag="early")
        x_word_table = keep.tile([P, T], U32, align_bytes=64, tag="x_words")
        d_word_table = keep.tile([P, G], U32, align_bytes=64)
        gs_t = keep.tile([P, PACK], F32)
        nc.gpsimd.memset(d_scale_table[:].bitcast(I32), 0)
        nc.gpsimd.dma_start(x_word_table[:].bitcast(I32), as_words(x_words))
        nc.gpsimd.dma_start(d_word_table[:].bitcast(I32), as_words(d_words))
        nc.gpsimd.dma_start(gs_t[:], gs.rearrange("(p t) o -> p (t o)", t=PACK))
        nc.scalar.dma_start(d_scale_table[0:P:8, :].bitcast(I32), d_scales[0].bitcast(I32))
        nc.vector.memset(x_scale_table[:].bitcast(I32), 0)
        for q in range(4):
            nc.scalar.dma_start(x_scale_table[32 * q : 32 * q + 4, :].bitcast(I32), x_scales[0, 4 * q : 4 * q + 4, :].bitcast(I32))
        k1_t = load_list("k1_t", k1)
        offs_t = load_list("offs_t", offs)
        k2_t = load_list("k2_t", k2)
        n1_t = load_list("n1_t", n1)
        n2_t = load_list("n2_t", n2)
        n3_t = load_list("n3_t", n3)
        n4_t = load_list("n4_t", n4)

        w1_scales = keep.tile([P, H], U8, align_bytes=64)
        nc.vector.memset(w1_scales[:].bitcast(I32), 0)
        win_a = [keep.tile([P, 2 * S], F32, name="win_a%d" % t, align_bytes=64) for t in range(PACK)]
        win_b = [keep.tile([P, 2 * S], F32, name="win_b%d" % t, align_bytes=64) for t in range(PACK)]

        gs2 = keep.tile([P, PACK], F32)
        nc.scalar.activation(gs2[:], gs_t[:], ACT.Copy, scale=2.0)

        def place_scales(dst, src, queues):
            for q, queue in enumerate(queues):
                queue.dma_start(dst[32 * q : 32 * q + 4, :].bitcast(I32), src[32 * q : 32 * q + 32 : 8, :].bitcast(I32))

        x_wd = keep.tile([P, S], U32, align_bytes=64)
        picked_s1 = keep.tile([P, H], U8, align_bytes=64)
        dealt_s1 = keep.tile([P, H], U8, align_bytes=64)
        nc.vector.tensor_copy(picked_s1[:], d_scale_table[:].indirect(k1_t[:]))
        nc.vector.tensor_copy(dealt_s1[:].rearrange("p (t m) -> p m t", t=PACK), picked_s1[:].rearrange("p (m t) -> p m t", t=PACK))
        place_scales(w1_scales, dealt_s1, (nc.sync,) * PACK)
        nc.vector.tensor_copy(x_wd[:], x_word_table[:].indirect(offs_t[:]))
        x_sc = keep.tile([P, S], U8, align_bytes=64)
        nc.vector.tensor_copy(x_sc[:], x_scale_table[:].indirect(offs_t[:]))
        picked_w = keep.tile([P, H], U32, align_bytes=64, tag="picked")
        nc.vector.tensor_copy(picked_w[:], d_word_table[:].indirect(k1_t[:]))
        w1_words = keep.tile([P, H], U32, align_bytes=64, tag="early")
        w2_words = keep.tile([P, H], U32, align_bytes=64)
        nc.vector.tensor_copy(w1_words[:].rearrange("p (t m) -> p m t", t=PACK), picked_w[:].rearrange("p (m t) -> p m t", t=PACK))

        ident = keep.tile([P, P], F32, align_bytes=64, tag="x_words")
        make_identity(nc, ident[:])
        bank = [psum.tile([P, S], F32, name="bank%d" % b) for b in range(8)]
        for t in range(PACK):
            cols = slice(P * t, P * (t + 1))
            nc.tensor.matmul_mx(out=bank[t][:], lhsT=w1_words[:, cols].bitcast(FP8X4), lhsT_scale=w1_scales[:, cols],
                                rhs=x_wd[:].bitcast(FP8X4), rhs_scale=x_sc[:], start=True, stop=True)

        nc.vector.tensor_copy(picked_w[:], d_word_table[:].indirect(k2_t[:]))
        nc.vector.tensor_copy(w2_words[:].rearrange("p (t u r) -> p u t r", t=PACK, r=LINE), picked_w[:].rearrange("p (u t r) -> p u t r", t=PACK, r=LINE))
        picked_s2 = keep.tile([P, H], U8, align_bytes=64, tag="picked")
        dealt_s2 = keep.tile([P, H], U8, align_bytes=64)
        nc.vector.tensor_copy(picked_s2[:], d_scale_table[:].indirect(k2_t[:]))
        nc.vector.tensor_copy(dealt_s2[:].bitcast(I32).rearrange("p (t u) -> p u t", t=PACK), picked_s2[:].bitcast(I32).rearrange("p (u t) -> p u t", t=PACK))

        def plane(name):
            return keep.tile([P, S], F32, name=name, align_bytes=64)

        def blocks(x):
            return [x[:, a:b] for a, b in QUARTERS]

        def blocks_of_halves(pair):
            return [half[:, a : a + P] for half in pair for a in range(0, HALF, P)]

        def add_turned(places, terms):
            for j, place in enumerate(places):
                for n, term in enumerate(terms):
                    nc.tensor.matmul(place, term[j], ident[:], is_transpose=True, start=n == 0, stop=n == len(terms) - 1)

        def turn(src, b):
            for block, place in zip(blocks(src), blocks(bank[b])):
                nc.tensor.transpose(place, block, ident[:])

        ex0 = plane("ex0")
        h3 = win_a[3][:, :S]
        ex = [ex0[:], win_a[1][:, :S], win_a[2][:, :S], win_a[3][:, S:]]
        ex_twin = {1: win_a[2][:, S:], 2: win_a[1][:, S:]}
        first_sum = {t: win_b[t][:, S:] for t in (1, 2)}
        ex0_both = win_b[0][:, S:]
        ex0_n1 = [first_sum[1][:, :HALF], first_sum[2][:, HALF:]]
        ex3_n1 = win_b[3][:, S:]
        den = {1: win_a[0][:, S:], 2: plane("den2")}
        ex3_n2 = keep.tile([P, S], F32, align_bytes=64, tag="late")
        root = [h3, plane("root_b")[:]]
        half_root = {1: root[1][:, :HALF], 2: root[1][:, HALF:]}
        inv_turned = keep.tile([P, 2, S], F32, align_bytes=64)
        inv = [inv_turned[:, 0, :], plane("inv1")[:], plane("inv2")[:], inv_turned[:, 1, :]]
        for t in range(3):
            nc.scalar.activation(ex[t], bank[t][:], ACT.Exp, scale=EXP_SCALE)
            if t in ex_twin:
                nc.sync.dma_start(ex_twin[t], ex[t])
        nc.scalar.activation(h3, bank[3][:], ACT.Copy, scale=EXP_SCALE)
        nc.scalar.activation(ex[3], bank[3][:], ACT.Exp, scale=EXP_SCALE)
        nc.scalar.activation(ex3_n1, win_a[3][:].indirect(n1_t[:]), ACT.Exp)
        nc.scalar.activation(ex3_n2[:], win_a[3][:].indirect(n2_t[:]), ACT.Exp)

        for (a, b), dst in zip(HALVES, ex0_n1):
            nc.vector.tensor_copy(dst, ex0[:].indirect(entries(n1_t, a, b)))
        for (a, b), src in zip(HALVES, ex0_n1):
            nc.vector.tensor_tensor(ex0_both[:, a:b], ex0[:].indirect(entries(n2_t, a, b)), src, ALU.add)

        sum_banks = (4, 6)
        add_turned(blocks_of_halves([bank[b][:, :HALF] for b in sum_banks]), [blocks(ex[0]), blocks(ex0_both)])
        add_turned(blocks_of_halves([bank[b][:, HALF:] for b in sum_banks]), [blocks(ex[3]), blocks(ex3_n1), blocks(ex3_n2)])
        for i, b in enumerate(sum_banks):
            nc.scalar.activation(root[i], bank[b][:], ACT.Abs_reciprocal_sqrt)
            turn(root[i], b + 1)
        for (lo, hi), b in zip(HALVES, sum_banks):
            nc.scalar.activation(inv_turned[:, :, lo:hi], bank[b + 1][:].rearrange("p (s j) -> p s j", s=2), ACT.Square)

        w2_scales = keep.tile([P, H], U8, align_bytes=64, tag="late")
        nc.gpsimd.memset(w2_scales[:].bitcast(I32), 0)
        place_scales(w2_scales, dealt_s2, (nc.sync,) * PACK)

        for t in (1, 2):
            nc.vector.tensor_tensor(first_sum[t], win_a[t][:].indirect(n1_t[:]), ex_twin[t], ALU.add)
        for a, b in HALVES:
            for t in (1, 2):
                nc.vector.tensor_tensor(den[t][:, a:b], win_a[t][:].indirect(entries(n2_t, a, b)), first_sum[t][:, a:b], ALU.add)
                nc.scalar.activation(half_root[t], den[t][:, a:b], ACT.Abs_reciprocal_sqrt)
                nc.scalar.activation(inv[t][:, a:b], half_root[t], ACT.Square)

        z_planes = [keep.tile([P, PACK, HALF], BF16, name="z_planes%d" % i, align_bytes=64) for i in range(2)]
        for pair in ((0, 3), (1, 2)):
            for i, (a, b) in enumerate(HALVES):
                for t in pair:
                    nc.vector.scalar_tensor_tensor(z_planes[i][:, t, :], ex[t][:, a:b], gs2[:, t : t + 1], inv[t][:, a:b], ALU.mult, ALU.mult)

        z_bf = [keep.tile([P, PACK * P], BF16, name="z_bf%d" % c, align_bytes=64) for c in range(len(QUARTERS))]
        z_wd = keep.tile([P, S], U32, align_bytes=64)
        z_sc = keep.tile([P, S], U8, align_bytes=64)

        def product(t, a, b):
            cols = slice(P * t, P * (t + 1))
            nc.tensor.matmul_mx(out=bank[H2_BANK[t][a // P]][:, a:b], lhsT=w2_words[:, cols].bitcast(FP8X4), lhsT_scale=w2_scales[:, cols],
                                rhs=z_wd[:, a:b].bitcast(FP8X4), rhs_scale=z_sc[:, a:b], start=True, stop=True)

        for c, (a, b) in enumerate(QUARTERS):
            i, lo = divmod(a, HALF)
            copy = nc.scalar.copy if b < S else nc.vector.tensor_copy
            copy(z_bf[c][:].rearrange("p (j i t) -> p j t i", i=LINE, t=PACK), z_planes[i][:, :, lo : lo + P].rearrange("p t (j i) -> p j t i", i=LINE))
        for c in (0, 1, 3, 2):
            a, b = QUARTERS[c]
            nc.vector.quantize_mx(out=z_wd[:, a:b].bitcast(FP8X4), scales=z_sc[:, a:b], in_=z_bf[c][:])
            product(1, a, b)
        for t in (0, 2, 3):
            product(t, 0, S)

        out_t = out.rearrange("(u t r) j -> t u r j", t=PACK, r=LINE)
        h2 = [win_a[t][:, :S] for t in range(PACK)]
        st = [win_b[t][:, :S] for t in range(PACK)]
        result = [plane("result%d" % t) for t in range(PACK)]
        twin = [plane("twin0")[:], plane("twin1")[:], st[3]]
        fetched = [plane("fetched%d" % t)[:] for t in range(3)] + [twin[1]]
        fetched_last = win_b[0][:, S:]
        turned = [fetched[2], plane("turned1")[:], plane("turned2")[:]]
        diff = [plane("diff%d" % t) for t in range(3)]
        excess = [[st[1][:, :HALF], st[2][:, :HALF]]]
        for whole in (plane("excess1"), turned[0]):
            excess.append([whole[:, a:b] for a, b in HALVES])
        turned_bank = (3, 5, 7)
        back_bank = (4, 6, 0)

        def leave_banks(t, sign, dsts):
            for b in sorted(set(H2_BANK[t])):
                mine = [quarter for quarter, its_bank in zip(QUARTERS, H2_BANK[t]) if its_bank == b]
                cols = slice(mine[0][0], mine[-1][1])
                for dst in dsts:
                    nc.scalar.activation(dst[:, cols], bank[b][:, cols], ACT.Copy, scale=sign * H_SCALE)

        def add_excess(t, base):
            for (a, b), dst in zip(HALVES, excess[t]):
                nc.scalar.activation(dst, diff[t][:, a:b], ACT.Relu)
            add_turned(blocks(bank[turned_bank[t]]), [blocks(base), blocks_of_halves(excess[t])])

        def turn_back(t):
            nc.scalar.copy(turned[t], bank[turned_bank[t]][:])
            turn(turned[t], back_bank[t])

        def store(t, a, b):
            nc.sync.dma_start(out_t[t, :, :, a:b], result[t][:, a:b])

        leave_banks(1, -1.0, (h2[1],))
        leave_banks(0, 1.0, (h2[0], twin[0]))
        leave_banks(2, -1.0, (h2[2],))
        nc.vector.tensor_copy(fetched[1], win_a[1][:].indirect(n3_t[:]))
        nc.vector.tensor_tensor(diff[0][:], win_a[0][:].indirect(n3_t[:]), twin[0], ALU.subtract)
        nc.vector.tensor_copy(fetched[2], win_a[2][:].indirect(n3_t[:]))
        add_excess(0, h2[0])
        leave_banks(3, 1.0, (h2[3],))
        for t in (1, 2):
            nc.vector.tensor_tensor(st[t], fetched[t], h2[t], ALU.min)
            nc.scalar.copy(twin[t], st[t])
        turn_back(0)
        nc.scalar.copy(st[0], bank[back_bank[0]][:])
        nc.vector.tensor_tensor(diff[1][:], win_b[1][:].indirect(n4_t[:]), twin[1], ALU.subtract)
        nc.vector.tensor_copy(fetched[3], win_a[3][:].indirect(n3_t[:]))
        nc.vector.tensor_tensor(diff[2][:], win_b[2][:].indirect(n4_t[:]), twin[2], ALU.subtract)
        nc.vector.tensor_tensor(st[3], fetched[3], h2[3], ALU.max)
        for t in (1, 2):
            add_excess(t, st[t])
        for t in (1, 2):
            turn_back(t)
        for t in (1, 2):
            nc.scalar.activation(result[t][:], bank[back_bank[t]][:], ACT.Copy, scale=-1.0)
            store(t, 0, S)

        nc.vector.tensor_copy(fetched[0], win_b[0][:].indirect(n4_t[:]))
        nc.vector.tensor_copy(fetched_last[:, :HALF], win_b[3][:].indirect(entries(n4_t, 0, HALF)))
        nc.vector.tensor_tensor(result[0][:], fetched[0], st[0], ALU.min)
        store(0, 0, S)
        nc.vector.tensor_copy(fetched_last[:, HALF:], win_b[3][:].indirect(entries(n4_t, HALF, S)))
        for a, b in HALVES:
            nc.vector.tensor_tensor(result[3][:, a:b], fetched_last[:, a:b], st[3][:, a:b], ALU.min)
            store(3, a, b)
